import numpy as np
import ml_dtypes


def mxq(x, axis, fmt="e4m3"):
    dtype, down = {"e4m3": (ml_dtypes.float8_e4m3fn, 7), "e5m2": (ml_dtypes.float8_e5m2, 14)}[fmt]
    v = np.moveaxis(np.asarray(x, np.float32).astype(ml_dtypes.bfloat16).astype(np.float64), axis, -1)
    blocks = v.reshape(v.shape[:-1] + (-1, 32))
    amax = np.abs(blocks).max(-1, keepdims=True)
    byte = np.maximum(np.where(amax > 0, np.frexp(amax)[1] - 1 + 127, 0) - down, 1)
    scale = np.exp2(byte - 127.0)
    codes = (blocks / scale).astype(np.float32).astype(dtype).astype(np.float64)
    return np.moveaxis((codes * scale).reshape(v.shape), -1, axis)


WIDE = False


def mx_kscale(k):
    if not WIDE:
        return np.ones(k)
    levels = np.array([30, -30])
    if k % 512:
        return np.exp2(np.random.permutation(np.resize(levels, k // 32))).repeat(32)
    a = np.empty((k // 512, 16))
    for p in range(k // 512):
        a[p, :8] = np.random.permutation(np.resize(levels, 8))
        for g in range(8):
            far = levels[np.abs(levels - a[p, g]) >= 10]
            a[p, g + 8] = far[np.random.randint(len(far))]
    return np.exp2(a.ravel()).repeat(32)


def f64(x):
    return np.asarray(x).astype(np.float64)


def striped(idx):
    return np.tile(np.asarray(idx).reshape(-1, 16).T, (8, 1)).astype(np.uint16)


def unstriped(offs):
    return offs[:16].T.reshape(-1).astype(np.int64)


E2M1 = np.array([0.0, 0.5, 1.0, 1.5, 2.0, 3.0, 4.0, 6.0, -0.0, -0.5, -1.0, -1.5, -2.0, -3.0, -4.0, -6.0])


def pack_weight(w, fmt):
    k, n = w.shape
    w = f64(np.asarray(w, np.float32).astype(ml_dtypes.bfloat16)).reshape(k // 32, 32, n)
    amax = np.abs(w).max(1)
    if fmt in ("e4m3", "e5m2"):
        byte = np.frexp(amax)[1] - 1 + 127 - (7 if fmt == "e4m3" else 14)
    else:
        mant, ex = np.frexp(amax / 6.0)
        byte = np.where(mant > 0.5, ex, ex - 1) + 127
    byte = np.clip(np.where(amax > 0, byte, 1), 1, 254)
    scaled = (w * np.exp2(127.0 - byte)[:, None, :]).reshape(k, n).astype(np.float32)
    by_word = np.ascontiguousarray(scaled.reshape(k // 512, 128, 4, n).transpose(0, 1, 3, 2))
    if fmt in ("e4m3", "e5m2"):
        words = by_word.astype(ml_dtypes.float8_e4m3fn if fmt == "e4m3" else ml_dtypes.float8_e5m2).view(np.uint8)
    else:
        c = by_word.astype(ml_dtypes.float4_e2m1fn).view(np.uint8) & 0xF
        words = (c[..., 0::2] | (c[..., 1::2] << 4)).reshape(k // 512, 128, 2 * n)
    return np.ascontiguousarray(words), np.ascontiguousarray(byte.astype(np.uint8).reshape(k // 512, 16, n))


def unpack_weight(words, scales, fmt):
    g, _, n = scales.shape
    words = np.ascontiguousarray(words).reshape(g, 128, n, -1)
    if fmt in ("e4m3", "e5m2"):
        vals = words.view(ml_dtypes.float8_e4m3fn if fmt == "e4m3" else ml_dtypes.float8_e5m2).astype(np.float64)
    else:
        nib = np.empty((g, 128, n, 4), np.uint8)
        nib[..., 0::2] = words & 0xF
        nib[..., 1::2] = words >> 4
        vals = E2M1[nib]
    vals = vals * np.repeat(np.exp2(scales.astype(np.float64) - 127.0), 8, axis=1)[..., None]
    return vals.transpose(0, 1, 3, 2).reshape(g * 512, n)


def sigmoid(v):
    return 1.0 / (1.0 + np.exp(-v))


K, T, Z, J, R, Q, N, L, E = 512, 1024, 1024, 256, 512, 1024, 256, 512, 1024


def setup_inputs():
    n = np.random.standard_normal
    idx = np.random.permutation(T)[:J]
    idx2 = np.random.permutation(Z)[:J]
    idx3 = np.random.permutation(Q)[:J]
    idx4 = np.random.permutation(E)[:J]
    fk = mx_kscale(K)
    fr = mx_kscale(R)
    fl = mx_kscale(L)
    xtp = pack_weight(n((K, T)) / fk[:, None], "e4m3")
    xop = pack_weight(n((K, Z)) / fk[:, None], "e2m1")
    wp = pack_weight(n((K, R)) * 1 / np.sqrt(K) * fk[:, None] * fr, "e5m2")
    w2p = pack_weight(n((K, R)) * 1 / np.sqrt(K) * fk[:, None] * fr, "e5m2")
    wbp = pack_weight(n((R, N)) * 1 / np.sqrt(R) / fr[:, None], "e5m2")
    sxp = pack_weight(n((L, J)) / fl[:, None], "e2m1")
    wsp = pack_weight(n((L, N)) * 1 / np.sqrt(L) * fl[:, None], "e5m2")
    return {
        "xt_words": xtp[0],
        "xt_scales": xtp[1],
        "xo_words": xop[0],
        "xo_scales": xop[1],
        "w_words": wp[0],
        "w_scales": wp[1],
        "w2_words": w2p[0],
        "w2_scales": w2p[1],
        "tg": (1.0 * n((R, Q))).astype(np.float32),
        "sg": (np.random.uniform(0.6, 1.6, (R, 1))).astype(np.float32),
        "bg": (np.random.uniform(-1.0, 1.0, (R, 1))).astype(np.float32),
        "wb_words": wbp[0],
        "wb_scales": wbp[1],
        "sx_words": sxp[0],
        "sx_scales": sxp[1],
        "ws_words": wsp[0],
        "ws_scales": wsp[1],
        "offs": striped(idx),
        "offs2": striped(idx2),
        "offs3": striped(idx3),
        "offs4": striped(idx4),
    }


def reference(xt_words, xt_scales, xo_words, xo_scales, w_words, w_scales, w2_words, w2_scales, tg, sg, bg, wb_words, wb_scales, sx_words, sx_scales, ws_words, ws_scales, offs, offs2, offs3, offs4):
    idx = unstriped(offs)
    idx2 = unstriped(offs2)
    idx3 = unstriped(offs3)
    idx4 = unstriped(offs4)
    xtu = unpack_weight(xt_words, xt_scales, "e4m3")
    xou = unpack_weight(xo_words, xo_scales, "e2m1")
    wu = unpack_weight(w_words, w_scales, "e5m2")
    w2u = unpack_weight(w2_words, w2_scales, "e5m2")
    wbu = unpack_weight(wb_words, wb_scales, "e5m2")
    sxu = unpack_weight(sx_words, sx_scales, "e2m1")
    wsu = unpack_weight(ws_words, ws_scales, "e5m2")
    xtidxg = xtu[:, idx]
    xoidx2g = xou[:, idx2]
    a = wu.T @ xtidxg + w2u.T @ xoidx2g
    b = w2u.T @ xtidxg + wu.T @ xoidx2g
    hid = np.abs(a - b) * sigmoid(f64(tg)[:, idx3] * f64(sg) + f64(bg))
    hidq = mxq(hid, 0, "e4m3")
    p = wbu.T @ hidq + wsu.T @ sxu
    y = np.zeros((N, E))
    y[:, idx4] = p
    return y

@@ -1,0 +1,216 @@
+from contextlib import ExitStack
+
+import concourse.mybir as mybir
+
+K, T, Z, J, R, Q, N, L, E = 512, 1024, 1024, 256, 512, 1024, 256, 512, 1024
+FLOPS = 2 * (4 * K * R * J + R * N * J + L * N * J)
+
+F32 = mybir.dt.float32
+BF16 = mybir.dt.bfloat16
+I32 = mybir.dt.int32
+U32 = mybir.dt.uint32
+U16 = mybir.dt.uint16
+U8 = mybir.dt.uint8
+E4M3 = mybir.dt.float8_e4m3fn_x4
+E5M2 = mybir.dt.float8_e5m2_x4
+E2M1 = mybir.dt.float4_e2m1fn_x4
+ALU = mybir.AluOpType
+ACT = mybir.ActivationFunctionType
+
+P = 128
+PACK = 4
+ROWS = 16
+C_XT, C_XO, C_W, C_W2 = 0, J, 2 * J, 2 * J + R
+C_END = 2 * J + 2 * R
+C_WB, C_WS, C_SX, C_LATE = 0, N, 2 * N, 2 * N + J
+
+
+def tile_list_crossed_tablegate_skip_scattered_kernel(
+    tc, xt_words, xt_scales, xo_words, xo_scales, w_words, w_scales, w2_words, w2_scales, tg, sg, bg,
+    wb_words, wb_scales, sx_words, sx_scales, ws_words, ws_scales, offs, offs2, offs3, offs4, out,
+):
+    nc = tc.nc
+
+    def words(ap):
+        return ap[0].rearrange("p n t -> p (n t)").bitcast(I32)
+
+    with ExitStack() as ctx:
+        lists = ctx.enter_context(tc.tile_pool(name="lists", bufs=1))
+        sb = ctx.enter_context(tc.tile_pool(name="sb", bufs=1))
+        psum = ctx.enter_context(tc.psum_pool(name="psum", bufs=1))
+
+        def tile(shape, dtype, name, tag=None):
+            return sb.tile(shape, dtype, name=name, tag=tag or name, align_bytes=64)
+
+        o1 = lists.tile([P, J // 16], U16, name="o1")
+        o2 = lists.tile([P, J // 16], U16, name="o2")
+        o3 = lists.tile([P, J // 16], U16, name="o3")
+        o4 = lists.tile([P, J // 16], U16, name="o4")
+
+        xt_s = tile([P, T], U8, "xt_s")
+        xo_s = tile([P, Z], U8, "xo_s")
+        planes = tile([P, C_END], U8, "planes")
+        nc.vector.memset(xt_s[:].bitcast(I32), 0)
+        nc.vector.memset(xo_s[:].bitcast(I32), 0)
+        nc.gpsimd.memset(planes[:, C_W:C_END].bitcast(I32), 0)
+        warm = tile([P, 2], F32, "warm")
+        nc.vector.memset(warm[:], 0.0)
+
+        def spread_rows(queue, rows):
+            for q in range(1, 4):
+                queue.dma_start(
+                    out=rows[32 * q : 32 * q + 4, :].bitcast(I32), in_=rows[4 * q : 4 * q + 4, :].bitcast(I32)
+                )
+
+        def load_rows(queue, dst, c0, scales):
+            queue.dma_start(out=dst[0:ROWS, c0 : c0 + scales.shape[2]].bitcast(I32), in_=scales[0].bitcast(I32))
+
+        load_rows(nc.scalar, xt_s, 0, xt_scales)
+        load_rows(nc.scalar, xo_s, 0, xo_scales)
+        nc.scalar.activation(out=warm[:, 1:2], in_=warm[:, 0:1], func=ACT.Sigmoid)
+
+        nc.sync.dma_start(o1[:], offs)
+        nc.sync.dma_start(o2[:], offs2)
+        nc.sync.dma_start(o3[:], offs3)
+        nc.sync.dma_start(o4[:], offs4)
+        xt_w = tile([P, T], U32, "xt_w", "slot_a")
+        xo_w = tile([P, Z], U16, "xo_w", "slot_b")
+        w_w = tile([P, 2 * R], U32, "w_w", "slot_e")
+        nc.sync.dma_start(out=xt_w[:].bitcast(I32), in_=words(xt_words))
+        nc.sync.dma_start(out=xo_w[:].bitcast(I32), in_=xo_words[0].bitcast(I32))
+        load_rows(nc.sync, planes, C_W, w_scales)
+        load_rows(nc.sync, planes, C_W2, w2_scales)
+        nc.sync.dma_start(out=w_w[:, 0:R].bitcast(I32), in_=words(w_words))
+        nc.sync.dma_start(out=w_w[:, R : 2 * R].bitcast(I32), in_=words(w2_words))
+
+        tg_rows = tg.rearrange("(p i) q -> p i q", i=PACK)
+        gates = {}
+
+        def load_gates(i, tag):
+            gates[i] = tile([P, Q], F32, f"tg{i}", tag)
+            nc.sync.dma_start(out=gates[i][:], in_=tg_rows[:, i, :])
+
+        load_gates(0, "slot_c")
+
+        slope = tile([P, PACK], F32, "slope")
+        offset = tile([P, PACK], F32, "offset")
+        nc.gpsimd.dma_start(out=slope[:], in_=sg.rearrange("(p i) o -> p (i o)", i=PACK))
+        nc.gpsimd.dma_start(out=offset[:], in_=bg.rearrange("(p i) o -> p (i o)", i=PACK))
+
+        pages = [tile([P, E], F32, f"page{h}") for h in range(2)]
+        for h in range(2):
+            nc.vector.memset(pages[h][:], 0.0)
+
+        xt_sg = tile([P, J], U8, "xt_sg", "slot_d")
+        xo_sg = tile([P, J], U8, "xo_sg")
+        nc.vector.tensor_copy(xt_sg[:], xt_s[:].indirect(o1[:]))
+        nc.vector.tensor_copy(xo_sg[:], xo_s[:].indirect(o2[:]))
+        nc.vector.tensor_copy(out=planes[:, C_XT : C_XT + J].bitcast(I32), in_=xt_sg[:].bitcast(I32))
+        nc.vector.tensor_copy(out=planes[:, C_XO : C_XO + J].bitcast(I32), in_=xo_sg[:].bitcast(I32))
+        spread_rows(nc.scalar, planes)
+        load_gates(1, "slot_d")
+
+        xt_g = tile([P, J], U32, "xt_g")
+        xo_g = tile([P, J], U16, "xo_g")
+        nc.vector.tensor_copy(xt_g[:], xt_w[:].indirect(o1[:]))
+        late_s = tile([P, C_LATE], U8, "late_s", "slot_a")
+        nc.gpsimd.memset(late_s[:].bitcast(I32), 0)
+        load_rows(nc.sync, late_s, C_WS, ws_scales)
+        load_rows(nc.sync, late_s, C_SX, sx_scales)
+        load_rows(nc.sync, late_s, C_WB, wb_scales)
+        nc.vector.tensor_copy(xo_g[:], xo_w[:].indirect(o2[:]))
+        load_gates(2, "slot_b")
+
+        w_p = [tile([P, 2 * P], U32, f"w_p{i}") for i in range(PACK)]
+        s_p = [tile([P, 2 * P], U8, f"s_p{i}") for i in range(PACK)]
+        for i in range(PACK):
+            nc.scalar.copy(out=w_p[i][:], in_=w_w[:].rearrange("p (m i) -> p i m", i=PACK)[:, i, :])
+            nc.vector.tensor_copy(
+                out=s_p[i][:], in_=planes[:, C_W:C_END].rearrange("p (m i) -> p i m", i=PACK)[:, i, :]
+            )
+
+        load_gates(3, "slot_e")
+        signed = tile([P, PACK, J], F32, "signed")
+
+        def first(bank, i, u):
+            for s, (codes, fmt, c0) in enumerate(((xt_g, E4M3, C_XT), (xo_g, E2M1, C_XO))):
+                v = (u + s) % 2
+                nc.tensor.matmul_mx(
+                    out=bank[:],
+                    lhsT=w_p[i][:, P * v : P * (v + 1)].bitcast(E5M2),
+                    lhsT_scale=s_p[i][:, P * v : P * (v + 1)],
+                    rhs=codes[:].bitcast(fmt),
+                    rhs_scale=planes[:, c0 : c0 + J],
+                    start=(s == 0),
+                    stop=(s == 1),
+                )
+
+        late_w = None
+        for i in range(PACK):
+            b_ps = psum.tile([P, J], F32, name=f"b_ps{i}", tag="b", bufs=3)
+            a_ps = psum.tile([P, J], F32, name=f"a_ps{i}", tag="a", bufs=3)
+            first(b_ps, i, 1)
+            first(a_ps, i, 0)
+            gate = tile([P, J], F32, f"gate{i}", f"b_sb{i - 2}" if i >= 2 else None)
+            nc.scalar.activation(
+                out=gate[:], in_=gates[i][:].indirect(o3[:]), func=ACT.Sigmoid,
+                bias=offset[:, i : i + 1], scale=slope[:, i : i + 1],
+            )
+            if i == 0:
+                late_w = tile([P, 2 * N + J // 2], U32, "late_w", "slot_c")
+                nc.sync.dma_start(out=late_w[:, N : 2 * N].bitcast(I32), in_=words(ws_words))
+                nc.sync.dma_start(out=late_w[:, 2 * N :].bitcast(I32), in_=sx_words[0].bitcast(I32))
+                nc.sync.dma_start(out=late_w[:, 0:N].bitcast(I32), in_=words(wb_words))
+                spread_rows(nc.sync, late_s)
+            b_sb = tile([P, J], F32, f"b_sb{i}")
+            nc.scalar.copy(out=b_sb[:], in_=b_ps[:])
+            diff = tile([P, J], F32, f"diff{i}")
+            nc.vector.tensor_tensor(diff[:], a_ps[:], b_sb[:], ALU.subtract)
+            nc.vector.tensor_tensor(signed[:, i, :], diff[:], gate[:], ALU.mult)
+
+        banks = {}
+        for g in range(2):
+            for h in range(2):
+                banks[g, h] = psum.tile([P, P], F32, name=f"p_ps{g}{h}", tag=("p", "ab"[h])[g], bufs=(2, 3)[g])
+                nc.tensor.matmul_mx(
+                    out=banks[g, h][:],
+                    lhsT=late_w[:, N + P * h : N + P * (h + 1)].bitcast(E5M2),
+                    lhsT_scale=late_s[:, C_WS + P * h : C_WS + P * (h + 1)],
+                    rhs=late_w[:, 2 * N + P // 2 * g : 2 * N + P // 2 * (g + 1)].bitcast(E2M1),
+                    rhs_scale=late_s[:, C_SX + P * g : C_SX + P * (g + 1)],
+                    start=True,
+                    stop=False,
+                )
+
+        for g in range(2):
+            woven = tile([P, P, PACK], BF16, f"woven{g}")
+            nc.scalar.activation(
+                out=woven[:].rearrange("p (c m) t -> p c t m", m=4),
+                in_=signed[:, :, P * g : P * (g + 1)].rearrange("p t (c m) -> p c t m", m=4),
+                func=ACT.Abs,
+            )
+            h_codes = tile([P, P], U32, f"h_codes{g}")
+            h_scales = tile([P, P], U8, f"h_scales{g}")
+            nc.vector.quantize_mx(
+                out=h_codes[:].bitcast(E4M3), scales=h_scales[:], in_=woven[:].rearrange("p c t -> p (c t)")
+            )
+            for h in range(2):
+                nc.tensor.matmul_mx(
+                    out=banks[g, h][:],
+                    lhsT=late_w[:, P * h : P * (h + 1)].bitcast(E5M2),
+                    lhsT_scale=late_s[:, C_WB + P * h : C_WB + P * (h + 1)],
+                    rhs=h_codes[:].bitcast(E4M3),
+                    rhs_scale=h_scales[:],
+                    start=False,
+                    stop=True,
+                )
+
+        for g in range(2):
+            places = o4[:, P // 16 * g : P // 16 * (g + 1)]
+            p_sb = [tile([P, P], F32, f"p_sb{g}{h}") for h in range(2)]
+            nc.scalar.copy(out=p_sb[0][:], in_=banks[g, 0][:])
+            nc.scalar.activation(out=pages[0][:].indirect(places), in_=p_sb[0][:], func=ACT.Copy)
+            nc.vector.tensor_copy(out=p_sb[1][:], in_=banks[g, 1][:])
+            nc.vector.tensor_copy(pages[1][:].indirect(places), p_sb[1][:])
+        for h in range(2):
+            nc.sync.dma_start(out=out[P * h : P * (h + 1), :], in_=pages[h][:])

@@ -21,7 +21,8 @@ P = 128
 PACK = 4
 ROWS = 16
 C_XT, C_XO, C_W, C_W2 = 0, J, 2 * J, 2 * J + R
-C_END = 2 * J + 2 * R
+C_FIRST = 2 * J + 2 * R
+C_END = C_FIRST + 2 * P
 C_WB, C_WS, C_SX, C_LATE = 0, N, 2 * N, 2 * N + J
 
 
@@ -50,38 +51,37 @@ def tile_list_crossed_tablegate_skip_scattered_kernel(
         xt_s = tile([P, T], U8, "xt_s")
         xo_s = tile([P, Z], U8, "xo_s")
         planes = tile([P, C_END], U8, "planes")
-        nc.vector.memset(xt_s[:].bitcast(I32), 0)
-        nc.vector.memset(xo_s[:].bitcast(I32), 0)
-        nc.gpsimd.memset(planes[:, C_W:C_END].bitcast(I32), 0)
         warm = tile([P, 2], F32, "warm")
         nc.vector.memset(warm[:], 0.0)
 
-        def spread_rows(queue, rows):
-            for q in range(1, 4):
-                queue.dma_start(
-                    out=rows[32 * q : 32 * q + 4, :].bitcast(I32), in_=rows[4 * q : 4 * q + 4, :].bitcast(I32)
-                )
+        def spread_rows(rows):
+            for r in range(1, 4):
+                nc.sync.dma_start(out=rows[r:P:32, :].bitcast(I32), in_=rows[8 * r : P : 32, :].bitcast(I32))
 
-        def load_rows(queue, dst, c0, scales):
-            queue.dma_start(out=dst[0:ROWS, c0 : c0 + scales.shape[2]].bitcast(I32), in_=scales[0].bitcast(I32))
+        def load_rows(dst, c0, scales):
+            width = scales.shape[2]
+            nc.sync.dma_start(
+                out=dst[:, c0 : c0 + width].bitcast(I32),
+                in_=scales[0].bitcast(I32).unsqueeze(1).broadcast_to([ROWS, P // ROWS, width // 4]),
+            )
 
-        load_rows(nc.scalar, xt_s, 0, xt_scales)
-        load_rows(nc.scalar, xo_s, 0, xo_scales)
         nc.scalar.activation(out=warm[:, 1:2], in_=warm[:, 0:1], func=ACT.Sigmoid)
 
         nc.sync.dma_start(o1[:], offs)
         nc.sync.dma_start(o2[:], offs2)
-        nc.sync.dma_start(o3[:], offs3)
-        nc.sync.dma_start(o4[:], offs4)
+        load_rows(planes, C_W, w_scales)
+        load_rows(planes, C_W2, w2_scales)
+        load_rows(xt_s, 0, xt_scales)
+        load_rows(xo_s, 0, xo_scales)
         xt_w = tile([P, T], U32, "xt_w", "slot_a")
         xo_w = tile([P, Z], U16, "xo_w", "slot_b")
-        w_w = tile([P, 2 * R], U32, "w_w", "slot_e")
+        w_w = [tile([P, R], U32, f"w_w{v}", f"slot_w{v}") for v in range(2)]
         nc.sync.dma_start(out=xt_w[:].bitcast(I32), in_=words(xt_words))
         nc.sync.dma_start(out=xo_w[:].bitcast(I32), in_=xo_words[0].bitcast(I32))
-        load_rows(nc.sync, planes, C_W, w_scales)
-        load_rows(nc.sync, planes, C_W2, w2_scales)
-        nc.sync.dma_start(out=w_w[:, 0:R].bitcast(I32), in_=words(w_words))
-        nc.sync.dma_start(out=w_w[:, R : 2 * R].bitcast(I32), in_=words(w2_words))
+        nc.sync.dma_start(o3[:], offs3)
+        nc.sync.dma_start(o4[:], offs4)
+        nc.sync.dma_start(out=w_w[0][:].bitcast(I32), in_=words(w_words))
+        nc.sync.dma_start(out=w_w[1][:].bitcast(I32), in_=words(w2_words))
 
         tg_rows = tg.rearrange("(p i) q -> p i q", i=PACK)
         gates = {}
@@ -92,86 +92,124 @@ def tile_list_crossed_tablegate_skip_scattered_kernel(
 
         load_gates(0, "slot_c")
 
-        slope = tile([P, PACK], F32, "slope")
-        offset = tile([P, PACK], F32, "offset")
-        nc.gpsimd.dma_start(out=slope[:], in_=sg.rearrange("(p i) o -> p (i o)", i=PACK))
-        nc.gpsimd.dma_start(out=offset[:], in_=bg.rearrange("(p i) o -> p (i o)", i=PACK))
-
         pages = [tile([P, E], F32, f"page{h}") for h in range(2)]
         for h in range(2):
             nc.vector.memset(pages[h][:], 0.0)
 
-        xt_sg = tile([P, J], U8, "xt_sg", "slot_d")
-        xo_sg = tile([P, J], U8, "xo_sg")
+        w_scale_cols = planes[:, C_W:C_FIRST].rearrange("p (m i) -> p i m", i=PACK)
+        nc.vector.tensor_copy(out=planes[:, C_FIRST:C_END], in_=w_scale_cols[:, 0, :])
+        xt_sg = tile([P, J], U8, "xt_sg")
+        xo_sg = tile([P, J], U8, "xo_sg", "slot_d")
         nc.vector.tensor_copy(xt_sg[:], xt_s[:].indirect(o1[:]))
         nc.vector.tensor_copy(xo_sg[:], xo_s[:].indirect(o2[:]))
         nc.vector.tensor_copy(out=planes[:, C_XT : C_XT + J].bitcast(I32), in_=xt_sg[:].bitcast(I32))
+        calib = tile([P, 16], F32, "calib", "xt_sg")
+        slope, offset = calib[:, 0:PACK], calib[:, 8 : 8 + PACK]
+        nc.sync.dma_start(out=slope, in_=sg.rearrange("(p i) o -> p (i o)", i=PACK))
+        nc.sync.dma_start(out=offset, in_=bg.rearrange("(p i) o -> p (i o)", i=PACK))
         nc.vector.tensor_copy(out=planes[:, C_XO : C_XO + J].bitcast(I32), in_=xo_sg[:].bitcast(I32))
-        spread_rows(nc.scalar, planes)
+        spread_rows(planes)
         load_gates(1, "slot_d")
 
         xt_g = tile([P, J], U32, "xt_g")
         xo_g = tile([P, J], U16, "xo_g")
         nc.vector.tensor_copy(xt_g[:], xt_w[:].indirect(o1[:]))
-        late_s = tile([P, C_LATE], U8, "late_s", "slot_a")
-        nc.gpsimd.memset(late_s[:].bitcast(I32), 0)
-        load_rows(nc.sync, late_s, C_WS, ws_scales)
-        load_rows(nc.sync, late_s, C_SX, sx_scales)
-        load_rows(nc.sync, late_s, C_WB, wb_scales)
+        load_gates(2, "slot_a")
         nc.vector.tensor_copy(xo_g[:], xo_w[:].indirect(o2[:]))
-        load_gates(2, "slot_b")
+        late_s = tile([P, C_LATE], U8, "late_s", "slot_b")
+        load_rows(late_s, C_WS, ws_scales)
+        load_rows(late_s, C_SX, sx_scales)
+        load_rows(late_s, C_WB, wb_scales)
 
-        w_p = [tile([P, 2 * P], U32, f"w_p{i}") for i in range(PACK)]
-        s_p = [tile([P, 2 * P], U8, f"s_p{i}") for i in range(PACK)]
-        for i in range(PACK):
-            nc.scalar.copy(out=w_p[i][:], in_=w_w[:].rearrange("p (m i) -> p i m", i=PACK)[:, i, :])
-            nc.vector.tensor_copy(
-                out=s_p[i][:], in_=planes[:, C_W:C_END].rearrange("p (m i) -> p i m", i=PACK)[:, i, :]
+        w_p = [tile([P, R], U32, f"w_p{v}") for v in range(2)]
+        for v in range(2):
+            nc.scalar.copy(
+                out=w_p[v][:].rearrange("p (i b m) -> p b i m", i=PACK, m=4),
+                in_=w_w[v][:].rearrange("p (b m i) -> p b i m", i=PACK, m=4),
             )
+        load_gates(3, "slot_w1")
 
-        load_gates(3, "slot_e")
-        signed = tile([P, PACK, J], F32, "signed")
+        s_p = [planes[:, C_FIRST:C_END]]
+        for i in range(1, PACK):
+            dealt = tile([P, 2 * P], U8, f"s_p{i}")
+            nc.vector.tensor_copy(out=dealt[:], in_=w_scale_cols[:, i, :])
+            s_p.append(dealt[:])
 
-        def first(bank, i, u):
+        def first(bank, i, u, g):
             for s, (codes, fmt, c0) in enumerate(((xt_g, E4M3, C_XT), (xo_g, E2M1, C_XO))):
                 v = (u + s) % 2
                 nc.tensor.matmul_mx(
-                    out=bank[:],
-                    lhsT=w_p[i][:, P * v : P * (v + 1)].bitcast(E5M2),
+                    out=bank,
+                    lhsT=w_p[v][:, P * i : P * (i + 1)].bitcast(E5M2),
                     lhsT_scale=s_p[i][:, P * v : P * (v + 1)],
-                    rhs=codes[:].bitcast(fmt),
-                    rhs_scale=planes[:, c0 : c0 + J],
+                    rhs=codes[:, P * g : P * (g + 1)].bitcast(fmt),
+                    rhs_scale=planes[:, c0 + P * g : c0 + P * (g + 1)],
                     start=(s == 0),
                     stop=(s == 1),
                 )
 
-        late_w = None
-        for i in range(PACK):
-            b_ps = psum.tile([P, J], F32, name=f"b_ps{i}", tag="b", bufs=3)
-            a_ps = psum.tile([P, J], F32, name=f"a_ps{i}", tag="a", bufs=3)
-            first(b_ps, i, 1)
-            first(a_ps, i, 0)
-            gate = tile([P, J], F32, f"gate{i}", f"b_sb{i - 2}" if i >= 2 else None)
+        gate = {}
+
+        def look(i, dst):
+            gate[i] = dst
             nc.scalar.activation(
-                out=gate[:], in_=gates[i][:].indirect(o3[:]), func=ACT.Sigmoid,
+                out=dst, in_=gates[i][:].indirect(o3[:]), func=ACT.Sigmoid,
                 bias=offset[:, i : i + 1], scale=slope[:, i : i + 1],
             )
-            if i == 0:
-                late_w = tile([P, 2 * N + J // 2], U32, "late_w", "slot_c")
-                nc.sync.dma_start(out=late_w[:, N : 2 * N].bitcast(I32), in_=words(ws_words))
-                nc.sync.dma_start(out=late_w[:, 2 * N :].bitcast(I32), in_=sx_words[0].bitcast(I32))
-                nc.sync.dma_start(out=late_w[:, 0:N].bitcast(I32), in_=words(wb_words))
-                spread_rows(nc.sync, late_s)
-            b_sb = tile([P, J], F32, f"b_sb{i}")
+
+        gated = [tile([P, PACK, P], BF16, "gated0"), tile([P, PACK, P], F32, "gated1")]
+        diff = {}
+
+        def difference(g, d):
+            b_ps = psum.tile([P, 2, P], F32, name=f"b_ps{g}{d}", tag=f"b{g}{d}")
+            a_ps = psum.tile([P, 2, P], F32, name=f"a_ps{g}{d}", tag=f"a{g}{d}")
+            for bank, u in ((b_ps, 1), (a_ps, 0)):
+                for e in range(2):
+                    first(bank[:, e, :], 2 * d + e, u, g)
+            b_sb = tile([P, 2, P], F32, f"b_sb{g}{d}")
             nc.scalar.copy(out=b_sb[:], in_=b_ps[:])
-            diff = tile([P, J], F32, f"diff{i}")
-            nc.vector.tensor_tensor(diff[:], a_ps[:], b_sb[:], ALU.subtract)
-            nc.vector.tensor_tensor(signed[:, i, :], diff[:], gate[:], ALU.mult)
+            diff[g, d] = tile([P, 2, P], F32, f"diff{g}{d}")
+            nc.vector.tensor_tensor(diff[g, d][:], a_ps[:], b_sb[:], ALU.subtract)
+            if g == 0:
+                size = tile([P, 2, P], F32, f"size{d}")
+                nc.vector.scalar_tensor_tensor(size[:], diff[g, d][:], -1.0, diff[g, d][:], ALU.mult, ALU.max)
+                diff[g, d] = size
+
+        def gate_pair(g):
+            nc.vector.tensor_tensor(
+                gated[g][:, 0:2, :], diff[g, 0][:], gate01[:, :, P * g : P * (g + 1)], ALU.mult
+            )
+
+        def gate_one(g, i):
+            nc.vector.tensor_tensor(
+                gated[g][:, i, :], diff[g, 1][:, i - 2, :], gate[i][:, P * g : P * (g + 1)], ALU.mult
+            )
+
+        gate01 = tile([P, 2, J], F32, "gate01")
+        look(0, gate01[:, 0, :])
+        late_w = tile([P, 2 * N + J // 2], U32, "late_w", "slot_c")
+        nc.sync.dma_start(out=late_w[:, N : 2 * N].bitcast(I32), in_=words(ws_words))
+        nc.sync.dma_start(out=late_w[:, 2 * N :].bitcast(I32), in_=sx_words[0].bitcast(I32))
+        nc.sync.dma_start(out=late_w[:, 0:N].bitcast(I32), in_=words(wb_words))
+        spread_rows(late_s)
+        difference(0, 0)
+        look(1, gate01[:, 1, :])
+        gate_pair(0)
+        difference(0, 1)
+        look(2, tile([P, J], F32, "gate2", "b_sb01")[:])
+        gate_one(0, 2)
+        difference(1, 0)
+        look(3, tile([P, J], F32, "gate3", "b_sb10")[:])
+        gate_one(0, 3)
+        gate_pair(1)
+        difference(1, 1)
+        gate_one(1, 2)
+        gate_one(1, 3)
 
         banks = {}
         for g in range(2):
             for h in range(2):
-                banks[g, h] = psum.tile([P, P], F32, name=f"p_ps{g}{h}", tag=("p", "ab"[h])[g], bufs=(2, 3)[g])
+                banks[g, h] = psum.tile([P, P], F32, name=f"p_ps{g}{h}", tag=f"{'ba'[h]}1{g}")
                 nc.tensor.matmul_mx(
                     out=banks[g, h][:],
                     lhsT=late_w[:, N + P * h : N + P * (h + 1)].bitcast(E5M2),
@@ -184,11 +222,12 @@ def tile_list_crossed_tablegate_skip_scattered_kernel(
 
         for g in range(2):
             woven = tile([P, P, PACK], BF16, f"woven{g}")
-            nc.scalar.activation(
-                out=woven[:].rearrange("p (c m) t -> p c t m", m=4),
-                in_=signed[:, :, P * g : P * (g + 1)].rearrange("p t (c m) -> p c t m", m=4),
-                func=ACT.Abs,
-            )
+            dst = woven[:].rearrange("p (c m) t -> p c t m", m=4)
+            src = gated[g][:].rearrange("p t (c m) -> p c t m", m=4)
+            if g == 0:
+                nc.vector.tensor_copy(out=dst, in_=src)
+            else:
+                nc.scalar.activation(out=dst, in_=src, func=ACT.Abs)
             h_codes = tile([P, P], U32, f"h_codes{g}")
             h_scales = tile([P, P], U8, f"h_scales{g}")
             nc.vector.quantize_mx(
@@ -205,12 +244,15 @@ def tile_list_crossed_tablegate_skip_scattered_kernel(
                     stop=True,
                 )
 
+        p_top = [tile([P, P], F32, f"p_top{g}") for g in range(2)]
+        p_low = tile([P, J], F32, "p_low")
         for g in range(2):
-            places = o4[:, P // 16 * g : P // 16 * (g + 1)]
-            p_sb = [tile([P, P], F32, f"p_sb{g}{h}") for h in range(2)]
-            nc.scalar.copy(out=p_sb[0][:], in_=banks[g, 0][:])
-            nc.scalar.activation(out=pages[0][:].indirect(places), in_=p_sb[0][:], func=ACT.Copy)
-            nc.vector.tensor_copy(out=p_sb[1][:], in_=banks[g, 1][:])
-            nc.vector.tensor_copy(pages[1][:].indirect(places), p_sb[1][:])
+            nc.vector.tensor_copy(out=p_top[g][:], in_=banks[g, 0][:])
+            nc.scalar.activation(
+                out=pages[0][:].indirect(o4[:, P // 16 * g : P // 16 * (g + 1)]), in_=p_top[g][:], func=ACT.Copy
+            )
+        for g in range(2):
+            nc.vector.tensor_copy(out=p_low[:, P * g : P * (g + 1)], in_=banks[g, 1][:])
+        nc.vector.tensor_copy(pages[1][:].indirect(o4[:]), p_low[:])
         for h in range(2):
             nc.sync.dma_start(out=out[P * h : P * (h + 1), :], in_=pages[h][:])

@@ -19,11 +19,17 @@ ACT = mybir.ActivationFunctionType
 
 P = 128
 PACK = 4
-ROWS = 16
+SCALE_ROWS = 16
+QUADRANT = 32
+PER_COLUMN = 16
+LINE = 4
+BIAS_AT = 8
+
 C_XT, C_XO, C_W, C_W2 = 0, J, 2 * J, 2 * J + R
-C_FIRST = 2 * J + 2 * R
-C_END = C_FIRST + 2 * P
-C_WB, C_WS, C_SX, C_LATE = 0, N, 2 * N, 2 * N + J
+C_SLICE0 = 2 * J + 2 * R
+C_END = C_SLICE0 + 2 * P
+C_WB, C_WS, C_SX, C_END2 = 0, N, 2 * N, 2 * N + J
+W_WB, W_WS, W_SX, W_END = 0, N, 2 * N, 2 * N + J // 2
 
 
 def tile_list_crossed_tablegate_skip_scattered_kernel(
@@ -32,7 +38,7 @@ def tile_list_crossed_tablegate_skip_scattered_kernel(
 ):
     nc = tc.nc
 
-    def words(ap):
+    def fp8_words(ap):
         return ap[0].rearrange("p n t -> p (n t)").bitcast(I32)
 
     with ExitStack() as ctx:
@@ -40,134 +46,139 @@ def tile_list_crossed_tablegate_skip_scattered_kernel(
         sb = ctx.enter_context(tc.tile_pool(name="sb", bufs=1))
         psum = ctx.enter_context(tc.psum_pool(name="psum", bufs=1))
 
-        def tile(shape, dtype, name, tag=None):
-            return sb.tile(shape, dtype, name=name, tag=tag or name, align_bytes=64)
+        def tile(shape, dtype, name, after=None):
+            return sb.tile(shape, dtype, name=name, tag=after or name, align_bytes=64)
 
-        o1 = lists.tile([P, J // 16], U16, name="o1")
-        o2 = lists.tile([P, J // 16], U16, name="o2")
-        o3 = lists.tile([P, J // 16], U16, name="o3")
-        o4 = lists.tile([P, J // 16], U16, name="o4")
+        tokens = lists.tile([P, J // PER_COLUMN], U16, name="tokens")
+        notes = lists.tile([P, J // PER_COLUMN], U16, name="notes")
+        entries = lists.tile([P, J // PER_COLUMN], U16, name="entries")
+        places = lists.tile([P, J // PER_COLUMN], U16, name="places")
 
         xt_s = tile([P, T], U8, "xt_s")
         xo_s = tile([P, Z], U8, "xo_s")
-        planes = tile([P, C_END], U8, "planes")
+        scales1 = tile([P, C_END], U8, "scales1")
+
         warm = tile([P, 2], F32, "warm")
         nc.vector.memset(warm[:], 0.0)
-
-        def spread_rows(rows):
-            for r in range(1, 4):
-                nc.sync.dma_start(out=rows[r:P:32, :].bitcast(I32), in_=rows[8 * r : P : 32, :].bitcast(I32))
-
-        def load_rows(dst, c0, scales):
-            width = scales.shape[2]
-            nc.sync.dma_start(
-                out=dst[:, c0 : c0 + width].bitcast(I32),
-                in_=scales[0].bitcast(I32).unsqueeze(1).broadcast_to([ROWS, P // ROWS, width // 4]),
-            )
-
         nc.scalar.activation(out=warm[:, 1:2], in_=warm[:, 0:1], func=ACT.Sigmoid)
 
-        nc.sync.dma_start(o1[:], offs)
-        nc.sync.dma_start(o2[:], offs2)
-        load_rows(planes, C_W, w_scales)
-        load_rows(planes, C_W2, w2_scales)
+        def load_rows(dst, c0, rows):
+            width = rows.shape[2]
+            nc.sync.dma_start(
+                out=dst[:, c0 : c0 + width].bitcast(I32),
+                in_=rows[0].bitcast(I32).unsqueeze(1).broadcast_to([SCALE_ROWS, P // SCALE_ROWS, width // 4]),
+            )
+
+        def spread_rows(rows):
+            for s in range(1, SCALE_ROWS * QUADRANT // P):
+                nc.sync.dma_start(
+                    out=rows[s:P:QUADRANT, :].bitcast(I32),
+                    in_=rows[P // SCALE_ROWS * s : P : QUADRANT, :].bitcast(I32),
+                )
+
+        nc.sync.dma_start(tokens[:], offs)
+        nc.sync.dma_start(notes[:], offs2)
+        load_rows(scales1, C_W, w_scales)
+        load_rows(scales1, C_W2, w2_scales)
         load_rows(xt_s, 0, xt_scales)
         load_rows(xo_s, 0, xo_scales)
-        xt_w = tile([P, T], U32, "xt_w", "slot_a")
-        xo_w = tile([P, Z], U16, "xo_w", "slot_b")
-        w_w = [tile([P, R], U32, f"w_w{v}", f"slot_w{v}") for v in range(2)]
-        nc.sync.dma_start(out=xt_w[:].bitcast(I32), in_=words(xt_words))
+        xt_w = tile([P, T], U32, "xt_w")
+        xo_w = tile([P, Z], U16, "xo_w")
+        w_w = [tile([P, R], U32, f"w_w{v}") for v in range(2)]
+        nc.sync.dma_start(out=xt_w[:].bitcast(I32), in_=fp8_words(xt_words))
         nc.sync.dma_start(out=xo_w[:].bitcast(I32), in_=xo_words[0].bitcast(I32))
-        nc.sync.dma_start(o3[:], offs3)
-        nc.sync.dma_start(o4[:], offs4)
-        nc.sync.dma_start(out=w_w[0][:].bitcast(I32), in_=words(w_words))
-        nc.sync.dma_start(out=w_w[1][:].bitcast(I32), in_=words(w2_words))
+        nc.sync.dma_start(entries[:], offs3)
+        nc.sync.dma_start(places[:], offs4)
+        nc.sync.dma_start(out=w_w[0][:].bitcast(I32), in_=fp8_words(w_words))
+        nc.sync.dma_start(out=w_w[1][:].bitcast(I32), in_=fp8_words(w2_words))
 
         tg_rows = tg.rearrange("(p i) q -> p i q", i=PACK)
-        gates = {}
+        table = {}
 
-        def load_gates(i, tag):
-            gates[i] = tile([P, Q], F32, f"tg{i}", tag)
-            nc.sync.dma_start(out=gates[i][:], in_=tg_rows[:, i, :])
+        def load_table(i, after):
+            table[i] = tile([P, Q], F32, f"table{i}", after)
+            nc.sync.dma_start(out=table[i][:], in_=tg_rows[:, i, :])
 
-        load_gates(0, "slot_c")
+        load_table(0, None)
 
         pages = [tile([P, E], F32, f"page{h}") for h in range(2)]
         for h in range(2):
             nc.vector.memset(pages[h][:], 0.0)
 
-        w_scale_cols = planes[:, C_W:C_FIRST].rearrange("p (m i) -> p i m", i=PACK)
-        nc.vector.tensor_copy(out=planes[:, C_FIRST:C_END], in_=w_scale_cols[:, 0, :])
+        w_scale_slices = scales1[:, C_W:C_SLICE0].rearrange("p (m i) -> p i m", i=PACK)
+        nc.vector.tensor_copy(out=scales1[:, C_SLICE0:C_END], in_=w_scale_slices[:, 0, :])
         xt_sg = tile([P, J], U8, "xt_sg")
-        xo_sg = tile([P, J], U8, "xo_sg", "slot_d")
-        nc.vector.tensor_copy(xt_sg[:], xt_s[:].indirect(o1[:]))
-        nc.vector.tensor_copy(xo_sg[:], xo_s[:].indirect(o2[:]))
-        nc.vector.tensor_copy(out=planes[:, C_XT : C_XT + J].bitcast(I32), in_=xt_sg[:].bitcast(I32))
-        calib = tile([P, 16], F32, "calib", "xt_sg")
-        slope, offset = calib[:, 0:PACK], calib[:, 8 : 8 + PACK]
+        xo_sg = tile([P, J], U8, "xo_sg")
+        nc.vector.tensor_copy(xt_sg[:], xt_s[:].indirect(tokens[:]))
+        nc.vector.tensor_copy(xo_sg[:], xo_s[:].indirect(notes[:]))
+        nc.vector.tensor_copy(out=scales1[:, C_XT : C_XT + J].bitcast(I32), in_=xt_sg[:].bitcast(I32))
+        affine = tile([P, 2 * BIAS_AT], F32, "affine", "xt_sg")
+        slope, bias = affine[:, 0:PACK], affine[:, BIAS_AT : BIAS_AT + PACK]
         nc.sync.dma_start(out=slope, in_=sg.rearrange("(p i) o -> p (i o)", i=PACK))
-        nc.sync.dma_start(out=offset, in_=bg.rearrange("(p i) o -> p (i o)", i=PACK))
-        nc.vector.tensor_copy(out=planes[:, C_XO : C_XO + J].bitcast(I32), in_=xo_sg[:].bitcast(I32))
-        spread_rows(planes)
-        load_gates(1, "slot_d")
+        nc.sync.dma_start(out=bias, in_=bg.rearrange("(p i) o -> p (i o)", i=PACK))
+        nc.vector.tensor_copy(out=scales1[:, C_XO : C_XO + J].bitcast(I32), in_=xo_sg[:].bitcast(I32))
+        spread_rows(scales1)
+        load_table(1, "xo_sg")
 
         xt_g = tile([P, J], U32, "xt_g")
         xo_g = tile([P, J], U16, "xo_g")
-        nc.vector.tensor_copy(xt_g[:], xt_w[:].indirect(o1[:]))
-        load_gates(2, "slot_a")
-        nc.vector.tensor_copy(xo_g[:], xo_w[:].indirect(o2[:]))
-        late_s = tile([P, C_LATE], U8, "late_s", "slot_b")
-        load_rows(late_s, C_WS, ws_scales)
-        load_rows(late_s, C_SX, sx_scales)
-        load_rows(late_s, C_WB, wb_scales)
+        nc.vector.tensor_copy(xt_g[:], xt_w[:].indirect(tokens[:]))
+        load_table(2, "xt_w")
+        nc.vector.tensor_copy(xo_g[:], xo_w[:].indirect(notes[:]))
+        scales2 = tile([P, C_END2], U8, "scales2", "xo_w")
+        load_rows(scales2, C_WS, ws_scales)
+        load_rows(scales2, C_SX, sx_scales)
+        load_rows(scales2, C_WB, wb_scales)
 
-        w_p = [tile([P, R], U32, f"w_p{v}") for v in range(2)]
+        w_dealt = [tile([P, R], U32, f"w_dealt{v}") for v in range(2)]
         for v in range(2):
             nc.scalar.copy(
-                out=w_p[v][:].rearrange("p (i b m) -> p b i m", i=PACK, m=4),
-                in_=w_w[v][:].rearrange("p (b m i) -> p b i m", i=PACK, m=4),
+                out=w_dealt[v][:].rearrange("p (i run nb) -> p run i nb", i=PACK, nb=LINE),
+                in_=w_w[v][:].rearrange("p (run nb i) -> p run i nb", i=PACK, nb=LINE),
             )
-        load_gates(3, "slot_w1")
+        load_table(3, "w_w1")
 
-        s_p = [planes[:, C_FIRST:C_END]]
+        s_dealt = [scales1[:, C_SLICE0:C_END]]
         for i in range(1, PACK):
-            dealt = tile([P, 2 * P], U8, f"s_p{i}")
-            nc.vector.tensor_copy(out=dealt[:], in_=w_scale_cols[:, i, :])
-            s_p.append(dealt[:])
+            s_slice = tile([P, 2 * P], U8, f"s_slice{i}")
+            nc.vector.tensor_copy(out=s_slice[:], in_=w_scale_slices[:, i, :])
+            s_dealt.append(s_slice[:])
 
-        def first(bank, i, u, g):
-            for s, (codes, fmt, c0) in enumerate(((xt_g, E4M3, C_XT), (xo_g, E2M1, C_XO))):
-                v = (u + s) % 2
+        def crossed_sum(bank, i, crossed, g):
+            for x, (codes, fmt, c0) in enumerate(((xt_g, E4M3, C_XT), (xo_g, E2M1, C_XO))):
+                v = (crossed + x) % 2
                 nc.tensor.matmul_mx(
                     out=bank,
-                    lhsT=w_p[v][:, P * i : P * (i + 1)].bitcast(E5M2),
-                    lhsT_scale=s_p[i][:, P * v : P * (v + 1)],
+                    lhsT=w_dealt[v][:, P * i : P * (i + 1)].bitcast(E5M2),
+                    lhsT_scale=s_dealt[i][:, P * v : P * (v + 1)],
                     rhs=codes[:, P * g : P * (g + 1)].bitcast(fmt),
-                    rhs_scale=planes[:, c0 + P * g : c0 + P * (g + 1)],
-                    start=(s == 0),
-                    stop=(s == 1),
+                    rhs_scale=scales1[:, c0 + P * g : c0 + P * (g + 1)],
+                    start=(x == 0),
+                    stop=(x == 1),
                 )
 
-        gate = {}
+        gate = {0: tile([P, 2, J], F32, "gate0")}
+        gated = [tile([P, PACK, P], BF16, "gated0"), tile([P, PACK, P], F32, "gated1")]
+        sums, diff, p_banks = {}, {}, {}
 
-        def look(i, dst):
-            gate[i] = dst
+        def look(i):
             nc.scalar.activation(
-                out=dst, in_=gates[i][:].indirect(o3[:]), func=ACT.Sigmoid,
-                bias=offset[:, i : i + 1], scale=slope[:, i : i + 1],
+                out=gate[i // 2][:, i % 2, :], in_=table[i][:].indirect(entries[:]), func=ACT.Sigmoid,
+                bias=bias[:, i : i + 1], scale=slope[:, i : i + 1],
             )
 
-        gated = [tile([P, PACK, P], BF16, "gated0"), tile([P, PACK, P], F32, "gated1")]
-        diff = {}
-
-        def difference(g, d):
+        def products(g, d):
             b_ps = psum.tile([P, 2, P], F32, name=f"b_ps{g}{d}", tag=f"b{g}{d}")
             a_ps = psum.tile([P, 2, P], F32, name=f"a_ps{g}{d}", tag=f"a{g}{d}")
-            for bank, u in ((b_ps, 1), (a_ps, 0)):
-                for e in range(2):
-                    first(bank[:, e, :], 2 * d + e, u, g)
+            for bank, crossed in ((b_ps, 1), (a_ps, 0)):
+                for odd in range(2):
+                    crossed_sum(bank[:, odd, :], 2 * d + odd, crossed, g)
+            sums[g, d] = a_ps, b_ps
+
+        def subtract(g, d, copy):
+            a_ps, b_ps = sums[g, d]
             b_sb = tile([P, 2, P], F32, f"b_sb{g}{d}")
-            nc.scalar.copy(out=b_sb[:], in_=b_ps[:])
+            copy(out=b_sb[:], in_=b_ps[:])
             diff[g, d] = tile([P, 2, P], F32, f"diff{g}{d}")
             nc.vector.tensor_tensor(diff[g, d][:], a_ps[:], b_sb[:], ALU.subtract)
             if g == 0:
@@ -175,84 +186,83 @@ def tile_list_crossed_tablegate_skip_scattered_kernel(
                 nc.vector.scalar_tensor_tensor(size[:], diff[g, d][:], -1.0, diff[g, d][:], ALU.mult, ALU.max)
                 diff[g, d] = size
 
-        def gate_pair(g):
+        def apply_gate(g, d, lo, hi):
             nc.vector.tensor_tensor(
-                gated[g][:, 0:2, :], diff[g, 0][:], gate01[:, :, P * g : P * (g + 1)], ALU.mult
+                gated[g][:, 2 * d + lo : 2 * d + hi, :],
+                diff[g, d][:, lo:hi, :],
+                gate[d][:, lo:hi, P * g : P * (g + 1)],
+                ALU.mult,
             )
 
-        def gate_one(g, i):
-            nc.vector.tensor_tensor(
-                gated[g][:, i, :], diff[g, 1][:, i - 2, :], gate[i][:, P * g : P * (g + 1)], ALU.mult
-            )
-
-        gate01 = tile([P, 2, J], F32, "gate01")
-        look(0, gate01[:, 0, :])
-        late_w = tile([P, 2 * N + J // 2], U32, "late_w", "slot_c")
-        nc.sync.dma_start(out=late_w[:, N : 2 * N].bitcast(I32), in_=words(ws_words))
-        nc.sync.dma_start(out=late_w[:, 2 * N :].bitcast(I32), in_=sx_words[0].bitcast(I32))
-        nc.sync.dma_start(out=late_w[:, 0:N].bitcast(I32), in_=words(wb_words))
-        spread_rows(late_s)
-        difference(0, 0)
-        look(1, gate01[:, 1, :])
-        gate_pair(0)
-        difference(0, 1)
-        look(2, tile([P, J], F32, "gate2", "b_sb01")[:])
-        gate_one(0, 2)
-        difference(1, 0)
-        look(3, tile([P, J], F32, "gate3", "b_sb10")[:])
-        gate_one(0, 3)
-        gate_pair(1)
-        difference(1, 1)
-        gate_one(1, 2)
-        gate_one(1, 3)
-
-        banks = {}
-        for g in range(2):
+        def second_stage(g):
             for h in range(2):
-                banks[g, h] = psum.tile([P, P], F32, name=f"p_ps{g}{h}", tag=f"{'ba'[h]}1{g}")
+                p_banks[g, h] = psum.tile([P, P], F32, name=f"p_ps{g}{h}", tag=f"{'ba'[h]}{1 - g}0")
                 nc.tensor.matmul_mx(
-                    out=banks[g, h][:],
-                    lhsT=late_w[:, N + P * h : N + P * (h + 1)].bitcast(E5M2),
-                    lhsT_scale=late_s[:, C_WS + P * h : C_WS + P * (h + 1)],
-                    rhs=late_w[:, 2 * N + P // 2 * g : 2 * N + P // 2 * (g + 1)].bitcast(E2M1),
-                    rhs_scale=late_s[:, C_SX + P * g : C_SX + P * (g + 1)],
+                    out=p_banks[g, h][:],
+                    lhsT=words2[:, W_WS + P * h : W_WS + P * (h + 1)].bitcast(E5M2),
+                    lhsT_scale=scales2[:, C_WS + P * h : C_WS + P * (h + 1)],
+                    rhs=words2[:, W_SX + P // 2 * g : W_SX + P // 2 * (g + 1)].bitcast(E2M1),
+                    rhs_scale=scales2[:, C_SX + P * g : C_SX + P * (g + 1)],
                     start=True,
                     stop=False,
                 )
-
-        for g in range(2):
             woven = tile([P, P, PACK], BF16, f"woven{g}")
-            dst = woven[:].rearrange("p (c m) t -> p c t m", m=4)
-            src = gated[g][:].rearrange("p t (c m) -> p c t m", m=4)
+            dst = woven[:].rearrange("p (run nb) i -> p run i nb", nb=LINE)
+            src = gated[g][:].rearrange("p i (run nb) -> p run i nb", nb=LINE)
             if g == 0:
                 nc.vector.tensor_copy(out=dst, in_=src)
             else:
                 nc.scalar.activation(out=dst, in_=src, func=ACT.Abs)
-            h_codes = tile([P, P], U32, f"h_codes{g}")
-            h_scales = tile([P, P], U8, f"h_scales{g}")
+            hid_words = tile([P, P], U32, f"hid_words{g}")
+            hid_scales = tile([P, P], U8, f"hid_scales{g}")
             nc.vector.quantize_mx(
-                out=h_codes[:].bitcast(E4M3), scales=h_scales[:], in_=woven[:].rearrange("p c t -> p (c t)")
+                out=hid_words[:].bitcast(E4M3), scales=hid_scales[:], in_=woven[:].rearrange("p j i -> p (j i)")
             )
             for h in range(2):
                 nc.tensor.matmul_mx(
-                    out=banks[g, h][:],
-                    lhsT=late_w[:, P * h : P * (h + 1)].bitcast(E5M2),
-                    lhsT_scale=late_s[:, C_WB + P * h : C_WB + P * (h + 1)],
-                    rhs=h_codes[:].bitcast(E4M3),
-                    rhs_scale=h_scales[:],
+                    out=p_banks[g, h][:],
+                    lhsT=words2[:, W_WB + P * h : W_WB + P * (h + 1)].bitcast(E5M2),
+                    lhsT_scale=scales2[:, C_WB + P * h : C_WB + P * (h + 1)],
+                    rhs=hid_words[:].bitcast(E4M3),
+                    rhs_scale=hid_scales[:],
                     start=False,
                     stop=True,
                 )
+            p_first = tile([P, P], F32, f"p_first{g}")
+            nc.vector.tensor_copy(out=p_first[:], in_=p_banks[g, 0][:])
+            half = places[:, P // PER_COLUMN * g : P // PER_COLUMN * (g + 1)]
+            nc.scalar.activation(out=pages[0][:].indirect(half), in_=p_first[:], func=ACT.Copy)
 
-        p_top = [tile([P, P], F32, f"p_top{g}") for g in range(2)]
-        p_low = tile([P, J], F32, "p_low")
+        look(0)
+        words2 = tile([P, W_END], U32, "words2", "table0")
+        nc.sync.dma_start(out=words2[:, W_WS:W_SX].bitcast(I32), in_=fp8_words(ws_words))
+        nc.sync.dma_start(out=words2[:, W_SX:W_END].bitcast(I32), in_=sx_words[0].bitcast(I32))
+        nc.sync.dma_start(out=words2[:, W_WB:W_WS].bitcast(I32), in_=fp8_words(wb_words))
+        spread_rows(scales2)
+
+        products(0, 0)
+        subtract(0, 0, nc.scalar.copy)
+        look(1)
+        apply_gate(0, 0, 0, 2)
+        products(1, 0)
+        subtract(1, 0, nc.scalar.copy)
+        apply_gate(1, 0, 0, 2)
+        products(0, 1)
+        products(1, 1)
+        subtract(0, 1, nc.vector.tensor_copy)
+        gate[1] = tile([P, 2, J], F32, "gate1", "b_sb10")
+        look(2)
+        apply_gate(0, 1, 0, 1)
+        look(3)
+        apply_gate(0, 1, 1, 2)
+        second_stage(0)
+        subtract(1, 1, nc.scalar.copy)
+        apply_gate(1, 1, 0, 2)
+        second_stage(1)
+
+        p_second = tile([P, J], F32, "p_second")
         for g in range(2):
-            nc.vector.tensor_copy(out=p_top[g][:], in_=banks[g, 0][:])
-            nc.scalar.activation(
-                out=pages[0][:].indirect(o4[:, P // 16 * g : P // 16 * (g + 1)]), in_=p_top[g][:], func=ACT.Copy
-            )
-        for g in range(2):
-            nc.vector.tensor_copy(out=p_low[:, P * g : P * (g + 1)], in_=banks[g, 1][:])
-        nc.vector.tensor_copy(pages[1][:].indirect(o4[:]), p_low[:])
+            nc.vector.tensor_copy(out=p_second[:, P * g : P * (g + 1)], in_=p_banks[g, 1][:])
+        nc.vector.tensor_copy(pages[1][:].indirect(places[:]), p_second[:])
         for h in range(2):
             nc.sync.dma_start(out=out[P * h : P * (h + 1), :], in_=pages[h][:])

from contextlib import ExitStack

import concourse.mybir as mybir

K, T, Z, J, R, Q, N, L, E = 512, 1024, 1024, 256, 512, 1024, 256, 512, 1024
FLOPS = 2 * (4 * K * R * J + R * N * J + L * N * J)

F32 = mybir.dt.float32
BF16 = mybir.dt.bfloat16
I32 = mybir.dt.int32
U32 = mybir.dt.uint32
U16 = mybir.dt.uint16
U8 = mybir.dt.uint8
E4M3 = mybir.dt.float8_e4m3fn_x4
E5M2 = mybir.dt.float8_e5m2_x4
E2M1 = mybir.dt.float4_e2m1fn_x4
ALU = mybir.AluOpType
ACT = mybir.ActivationFunctionType

P = 128
PACK = 4
SCALE_ROWS = 16
QUADRANT = 32
PER_COLUMN = 16
LINE = 4
BIAS_AT = 8

C_XT, C_XO, C_W, C_W2 = 0, J, 2 * J, 2 * J + R
C_SLICE0 = 2 * J + 2 * R
C_END = C_SLICE0 + 2 * P
C_WB, C_WS, C_SX, C_END2 = 0, N, 2 * N, 2 * N + J
W_WB, W_WS, W_SX, W_END = 0, N, 2 * N, 2 * N + J // 2


def tile_list_crossed_tablegate_skip_scattered_kernel(
    tc, xt_words, xt_scales, xo_words, xo_scales, w_words, w_scales, w2_words, w2_scales, tg, sg, bg,
    wb_words, wb_scales, sx_words, sx_scales, ws_words, ws_scales, offs, offs2, offs3, offs4, out,
):
    nc = tc.nc

    def fp8_words(ap):
        return ap[0].rearrange("p n t -> p (n t)").bitcast(I32)

    with ExitStack() as ctx:
        lists = ctx.enter_context(tc.tile_pool(name="lists", bufs=1))
        sb = ctx.enter_context(tc.tile_pool(name="sb", bufs=1))
        psum = ctx.enter_context(tc.psum_pool(name="psum", bufs=1))

        def tile(shape, dtype, name, after=None):
            return sb.tile(shape, dtype, name=name, tag=after or name, align_bytes=64)

        tokens = lists.tile([P, J // PER_COLUMN], U16, name="tokens")
        notes = lists.tile([P, J // PER_COLUMN], U16, name="notes")
        entries = lists.tile([P, J // PER_COLUMN], U16, name="entries")
        places = lists.tile([P, J // PER_COLUMN], U16, name="places")

        xt_s = tile([P, T], U8, "xt_s")
        xo_s = tile([P, Z], U8, "xo_s")
        scales1 = tile([P, C_END], U8, "scales1")

        warm = tile([P, 2], F32, "warm")
        nc.vector.memset(warm[:], 0.0)
        nc.scalar.activation(out=warm[:, 1:2], in_=warm[:, 0:1], func=ACT.Sigmoid)

        def load_rows(dst, c0, rows):
            width = rows.shape[2]
            nc.sync.dma_start(
                out=dst[:, c0 : c0 + width].bitcast(I32),
                in_=rows[0].bitcast(I32).unsqueeze(1).broadcast_to([SCALE_ROWS, P // SCALE_ROWS, width // 4]),
            )

        def spread_rows(rows):
            for s in range(1, SCALE_ROWS * QUADRANT // P):
                nc.sync.dma_start(
                    out=rows[s:P:QUADRANT, :].bitcast(I32),
                    in_=rows[P // SCALE_ROWS * s : P : QUADRANT, :].bitcast(I32),
                )

        nc.sync.dma_start(tokens[:], offs)
        nc.sync.dma_start(notes[:], offs2)
        load_rows(scales1, C_W, w_scales)
        load_rows(scales1, C_W2, w2_scales)
        load_rows(xt_s, 0, xt_scales)
        load_rows(xo_s, 0, xo_scales)
        xt_w = tile([P, T], U32, "xt_w")
        xo_w = tile([P, Z], U16, "xo_w")
        w_w = [tile([P, R], U32, f"w_w{v}") for v in range(2)]
        nc.sync.dma_start(out=xt_w[:].bitcast(I32), in_=fp8_words(xt_words))
        nc.sync.dma_start(out=xo_w[:].bitcast(I32), in_=xo_words[0].bitcast(I32))
        nc.sync.dma_start(entries[:], offs3)
        nc.sync.dma_start(places[:], offs4)
        nc.sync.dma_start(out=w_w[0][:].bitcast(I32), in_=fp8_words(w_words))
        nc.sync.dma_start(out=w_w[1][:].bitcast(I32), in_=fp8_words(w2_words))

        tg_rows = tg.rearrange("(p i) q -> p i q", i=PACK)
        table = {}

        def load_table(i, after):
            table[i] = tile([P, Q], F32, f"table{i}", after)
            nc.sync.dma_start(out=table[i][:], in_=tg_rows[:, i, :])

        load_table(0, None)

        pages = [tile([P, E], F32, f"page{h}") for h in range(2)]
        for h in range(2):
            nc.vector.memset(pages[h][:], 0.0)

        w_scale_slices = scales1[:, C_W:C_SLICE0].rearrange("p (m i) -> p i m", i=PACK)
        nc.vector.tensor_copy(out=scales1[:, C_SLICE0:C_END], in_=w_scale_slices[:, 0, :])
        xt_sg = tile([P, J], U8, "xt_sg")
        xo_sg = tile([P, J], U8, "xo_sg")
        nc.vector.tensor_copy(xt_sg[:], xt_s[:].indirect(tokens[:]))
        nc.vector.tensor_copy(xo_sg[:], xo_s[:].indirect(notes[:]))
        nc.vector.tensor_copy(out=scales1[:, C_XT : C_XT + J].bitcast(I32), in_=xt_sg[:].bitcast(I32))
        affine = tile([P, 2 * BIAS_AT], F32, "affine", "xt_sg")
        slope, bias = affine[:, 0:PACK], affine[:, BIAS_AT : BIAS_AT + PACK]
        nc.sync.dma_start(out=slope, in_=sg.rearrange("(p i) o -> p (i o)", i=PACK))
        nc.sync.dma_start(out=bias, in_=bg.rearrange("(p i) o -> p (i o)", i=PACK))
        nc.vector.tensor_copy(out=scales1[:, C_XO : C_XO + J].bitcast(I32), in_=xo_sg[:].bitcast(I32))
        spread_rows(scales1)
        load_table(1, "xo_sg")

        xt_g = tile([P, J], U32, "xt_g")
        xo_g = tile([P, J], U16, "xo_g")
        nc.vector.tensor_copy(xt_g[:], xt_w[:].indirect(tokens[:]))
        load_table(2, "xt_w")
        nc.vector.tensor_copy(xo_g[:], xo_w[:].indirect(notes[:]))
        scales2 = tile([P, C_END2], U8, "scales2", "xo_w")
        load_rows(scales2, C_WS, ws_scales)
        load_rows(scales2, C_SX, sx_scales)
        load_rows(scales2, C_WB, wb_scales)

        w_dealt = [tile([P, R], U32, f"w_dealt{v}") for v in range(2)]
        for v in range(2):
            nc.scalar.copy(
                out=w_dealt[v][:].rearrange("p (i run nb) -> p run i nb", i=PACK, nb=LINE),
                in_=w_w[v][:].rearrange("p (run nb i) -> p run i nb", i=PACK, nb=LINE),
            )
        load_table(3, "w_w1")

        s_dealt = [scales1[:, C_SLICE0:C_END]]
        for i in range(1, PACK):
            s_slice = tile([P, 2 * P], U8, f"s_slice{i}")
            nc.vector.tensor_copy(out=s_slice[:], in_=w_scale_slices[:, i, :])
            s_dealt.append(s_slice[:])

        def crossed_sum(bank, i, crossed, g):
            for x, (codes, fmt, c0) in enumerate(((xt_g, E4M3, C_XT), (xo_g, E2M1, C_XO))):
                v = (crossed + x) % 2
                nc.tensor.matmul_mx(
                    out=bank,
                    lhsT=w_dealt[v][:, P * i : P * (i + 1)].bitcast(E5M2),
                    lhsT_scale=s_dealt[i][:, P * v : P * (v + 1)],
                    rhs=codes[:, P * g : P * (g + 1)].bitcast(fmt),
                    rhs_scale=scales1[:, c0 + P * g : c0 + P * (g + 1)],
                    start=(x == 0),
                    stop=(x == 1),
                )

        gate = {0: tile([P, 2, J], F32, "gate0")}
        gated = [tile([P, PACK, P], BF16, "gated0"), tile([P, PACK, P], F32, "gated1")]
        sums, diff, p_banks = {}, {}, {}

        def look(i):
            nc.scalar.activation(
                out=gate[i // 2][:, i % 2, :], in_=table[i][:].indirect(entries[:]), func=ACT.Sigmoid,
                bias=bias[:, i : i + 1], scale=slope[:, i : i + 1],
            )

        def products(g, d):
            b_ps = psum.tile([P, 2, P], F32, name=f"b_ps{g}{d}", tag=f"b{g}{d}")
            a_ps = psum.tile([P, 2, P], F32, name=f"a_ps{g}{d}", tag=f"a{g}{d}")
            for bank, crossed in ((b_ps, 1), (a_ps, 0)):
                for odd in range(2):
                    crossed_sum(bank[:, odd, :], 2 * d + odd, crossed, g)
            sums[g, d] = a_ps, b_ps

        def subtract(g, d, copy):
            a_ps, b_ps = sums[g, d]
            b_sb = tile([P, 2, P], F32, f"b_sb{g}{d}")
            copy(out=b_sb[:], in_=b_ps[:])
            diff[g, d] = tile([P, 2, P], F32, f"diff{g}{d}")
            nc.vector.tensor_tensor(diff[g, d][:], a_ps[:], b_sb[:], ALU.subtract)
            if g == 0:
                size = tile([P, 2, P], F32, f"size{d}")
                nc.vector.scalar_tensor_tensor(size[:], diff[g, d][:], -1.0, diff[g, d][:], ALU.mult, ALU.max)
                diff[g, d] = size

        def apply_gate(g, d, lo, hi):
            nc.vector.tensor_tensor(
                gated[g][:, 2 * d + lo : 2 * d + hi, :],
                diff[g, d][:, lo:hi, :],
                gate[d][:, lo:hi, P * g : P * (g + 1)],
                ALU.mult,
            )

        def second_stage(g):
            for h in range(2):
                p_banks[g, h] = psum.tile([P, P], F32, name=f"p_ps{g}{h}", tag=f"{'ba'[h]}{1 - g}0")
                nc.tensor.matmul_mx(
                    out=p_banks[g, h][:],
                    lhsT=words2[:, W_WS + P * h : W_WS + P * (h + 1)].bitcast(E5M2),
                    lhsT_scale=scales2[:, C_WS + P * h : C_WS + P * (h + 1)],
                    rhs=words2[:, W_SX + P // 2 * g : W_SX + P // 2 * (g + 1)].bitcast(E2M1),
                    rhs_scale=scales2[:, C_SX + P * g : C_SX + P * (g + 1)],
                    start=True,
                    stop=False,
                )
            woven = tile([P, P, PACK], BF16, f"woven{g}")
            dst = woven[:].rearrange("p (run nb) i -> p run i nb", nb=LINE)
            src = gated[g][:].rearrange("p i (run nb) -> p run i nb", nb=LINE)
            if g == 0:
                nc.vector.tensor_copy(out=dst, in_=src)
            else:
                nc.scalar.activation(out=dst, in_=src, func=ACT.Abs)
            hid_words = tile([P, P], U32, f"hid_words{g}")
            hid_scales = tile([P, P], U8, f"hid_scales{g}")
            nc.vector.quantize_mx(
                out=hid_words[:].bitcast(E4M3), scales=hid_scales[:], in_=woven[:].rearrange("p j i -> p (j i)")
            )
            for h in range(2):
                nc.tensor.matmul_mx(
                    out=p_banks[g, h][:],
                    lhsT=words2[:, W_WB + P * h : W_WB + P * (h + 1)].bitcast(E5M2),
                    lhsT_scale=scales2[:, C_WB + P * h : C_WB + P * (h + 1)],
                    rhs=hid_words[:].bitcast(E4M3),
                    rhs_scale=hid_scales[:],
                    start=False,
                    stop=True,
                )
            p_first = tile([P, P], F32, f"p_first{g}")
            nc.vector.tensor_copy(out=p_first[:], in_=p_banks[g, 0][:])
            half = places[:, P // PER_COLUMN * g : P // PER_COLUMN * (g + 1)]
            nc.scalar.activation(out=pages[0][:].indirect(half), in_=p_first[:], func=ACT.Copy)

        look(0)
        words2 = tile([P, W_END], U32, "words2", "table0")
        nc.sync.dma_start(out=words2[:, W_WS:W_SX].bitcast(I32), in_=fp8_words(ws_words))
        nc.sync.dma_start(out=words2[:, W_SX:W_END].bitcast(I32), in_=sx_words[0].bitcast(I32))
        nc.sync.dma_start(out=words2[:, W_WB:W_WS].bitcast(I32), in_=fp8_words(wb_words))
        spread_rows(scales2)

        products(0, 0)
        subtract(0, 0, nc.scalar.copy)
        look(1)
        apply_gate(0, 0, 0, 2)
        products(1, 0)
        subtract(1, 0, nc.scalar.copy)
        apply_gate(1, 0, 0, 2)
        products(0, 1)
        products(1, 1)
        subtract(0, 1, nc.vector.tensor_copy)
        gate[1] = tile([P, 2, J], F32, "gate1", "b_sb10")
        look(2)
        apply_gate(0, 1, 0, 1)
        look(3)
        apply_gate(0, 1, 1, 2)
        second_stage(0)
        subtract(1, 1, nc.scalar.copy)
        apply_gate(1, 1, 0, 2)
        second_stage(1)

        p_second = tile([P, J], F32, "p_second")
        for g in range(2):
            nc.vector.tensor_copy(out=p_second[:, P * g : P * (g + 1)], in_=p_banks[g, 1][:])
        nc.vector.tensor_copy(pages[1][:].indirect(places[:]), p_second[:])
        for h in range(2):
            nc.sync.dma_start(out=out[P * h : P * (h + 1), :], in_=pages[h][:])
